import numpy as np, ml_dtypes
CORES = [10,34,74,98]
N = 4
import mx_ref
NC, G, MB = 128, 2, 3
C = np.float32(0.047)
BF = ml_dtypes.bfloat16
def cut(t, i, w=512):
    return t[:, w * i:w * i + w]
def tile(rs):
    return np.stack(rs, axis=2).reshape(128, -1).astype(BF)
def layer(w, X):
    out = []
    for i in range(G):
        for t in range(len(X)):
            p = mx_ref.matmul(mx_ref.quantize(cut(w, len(X) * i + t)), X[t])
            z = p if t == 0 else z + p
        out.append(z)
    return out
def act(Z):
    return [np.maximum(s * z, 0) * C for z in Z for s in (1, -1)]
def setup_inputs(rng):
    def f(*shape):
        return mx_ref.flush((rng.standard_normal(shape, dtype=np.float32) * np.exp2(rng.integers(-2, 3, shape[:-1] + (1,)))).astype(BF))
    return {"x": f(N, 128, 4 * NC), "w1": f(N, 128, G * 512), "w2": f(N, 128, 512), "px": f(N, 128, MB * 4 * NC), "pw": f(N, 128, G * 512)}
def setup_inputs_blocks(rng):
    d = setup_inputs(rng)
    for k in ("x", "w1", "w2", "px"): d[k] = mx_ref.spread(d[k], rng, 4)
    for k in ("pw",): d[k] = mx_ref.spread(d[k], rng, 1)
    return d
def setup_inputs_wide(rng):
    d = setup_inputs(rng)
    for k in ("x", "w1", "w2", "px"): d[k] = mx_ref.flush((d[k].astype(np.float32) * np.exp2(rng.integers(-6, 7, (N, 1, 1))).astype(np.float32)).astype(BF))
    return d
def setup_inputs_zeros(rng):
    d = setup_inputs(rng); v = d["x"].reshape(N, 128, -1, 4).copy()
    v[np.broadcast_to((rng.random((N, 1, v.shape[2], 1)) < 0.33), v.shape)] = 0
    d["x"] = v.reshape(d["x"].shape)
    return d
def reference(x, w1, w2, px, pw):
    H = [mx_ref.quantize(tile(act(layer(w1[j], [mx_ref.quantize(x[j])])))) for j in range(N)]
    y = np.zeros((N, 128, N * NC), np.float32)
    for r in range(N):
        qw = mx_ref.quantize(w2[r])
        for j in range(N):
            y[r][:, NC * j:NC * j + NC] = mx_ref.matmul(qw, H[j])
    z = np.full((N, 128, MB * G * NC), np.nan, np.float32)
    for m in range(MB):
        a = mx_ref.quantize(cut(px[N - 1], m, 4 * NC))
        for s in range(N - 1):
            a = mx_ref.quantize(tile(act(layer(pw[s], [a]))))
        Z = layer(pw[N - 1], [a])
        for i in range(G):
            z[N - 1][:, NC * (G * m + i):NC * (G * m + i) + NC] = Z[i]
    return {"y": y, "z": z}

import numpy as np
from concourse.bass import DstId, RemoteDMATransfer
from concourse.mybir import dt, AluOpType, ActivationFunctionType

CODES = "float8_e4m3fn_x4"
C = float(np.float32(0.047))
H = 192
LAST = 3

SCRATCH = {
    "bx": ("sbuf", [128, 512], "bfloat16"),
    "bw1": ("sbuf", [128, 1024], "bfloat16"),
    "bw2": ("sbuf", [128, 512], "bfloat16"),
    "bpw": ("sbuf", [128, 1024], "bfloat16"),
    "bpx": ("sbuf", [128, 1536], "bfloat16"),
    "qx": ("sbuf", [128, 128], CODES), "sx": ("sbuf", [128, 128], "uint8"),
    "qw1": ("sbuf", [128, 256], CODES), "sw1": ("sbuf", [128, 256], "uint8"),
    "qw2": ("sbuf", [128, 128], CODES), "sw2": ("sbuf", [128, 128], "uint8"),
    "qpw": ("sbuf", [128, 256], CODES), "spw": ("sbuf", [128, 256], "uint8"),
    "qpx": ("sbuf", [128, 384], CODES), "spx": ("sbuf", [128, 384], "uint8"),
    "rpw": ("sbuf", [128, 256], CODES), "rspw": ("sbuf", [128, 256], "uint8"),
    "th": ("sbuf", [128, 512], "bfloat16"),
    "hq": ("sbuf", [128, 512], CODES), "hs": ("sbuf", [128, 512], "uint8"),
    "rq": ("sbuf", [128, 384], CODES), "rs": ("sbuf", [128, 384], "uint8"),
    "t0": ("sbuf", [128, 768], "bfloat16"), "t1": ("sbuf", [128, 768], "bfloat16"),
    "q0": ("sbuf", [128, H], CODES), "s0": ("sbuf", [128, H], "uint8"),
    "q1": ("sbuf", [128, H], CODES), "s1": ("sbuf", [128, H], "uint8"),
    "ysb": ("sbuf", [128, 512], "float32"),
    "zsb": ("sbuf", [128, 768], "float32"),
    "ph0": ("psum", [128, 512], "float32"), "ph1": ("psum", [128, 512], "float32"),
    "pa0": ("psum", [128, 512], "float32"), "pa1": ("psum", [128, 512], "float32"),
    "pb0": ("psum", [128, 512], "float32"), "pb1": ("psum", [128, 512], "float32"),
    "py0": ("psum", [128, 512], "float32"), "py1": ("psum", [128, 512], "float32"),
}

SEMAPHORES = (
    ["lx", "lw1", "lw2", "lpw", "lpxa", "lpxb"]
    + ["kx", "kw1", "kw2", "kpw", "kpxa", "kpxb"]
    + [p + k for k in ("h", "a", "b") for p in ("m0", "m1", "sc", "ve", "k")]
    + ["ina", "ins", "inb", "inw", "h0", "h1", "h2", "h3"]
    + ["senta", "sent"]
    + ["my0", "my1", "cy", "sty", "mz0", "mz1", "mz2", "mz3", "cza", "czb", "stz"]
)


def rank_program(g, core, T, topo):
    rank = T.rank_of(core)
    if rank is None:
        return
    sem = T.sem
    nsent = [0]

    def u8(view):
        return view.bitcast(dt.uint8)

    def bits(mask):
        return bin(mask).count("1")

    def send(src, dst, ranks, rsem, lsem=None):
        cores = [T.cores[r] for r in ranks]
        mask = topo.mask(core, cores[0])
        for c in cores:
            assert topo.may_write(core, c)
            mask &= topo.mask(core, c)
        if lsem is None:
            lsem = sem.sent
            nsent[0] += bits(mask)
        if len(cores) == 1:
            rid, pid, _ = topo.addr(cores[0])
            g.remote_dma(dst, src, rsem, lsem, pid, rid, mask)
        else:
            ids = [DstId(rid=topo.addr(c)[0], pnc=topo.addr(c)[1]) for c in cores]
            g.remote_dma_fused([RemoteDMATransfer(dst_ids=ids, dma_engine_mask=mask, remote_sem=rsem,
                                                  srcs=[src], dsts=[dst for _ in cores])], local_sem=lsem)
        return bits(mask)

    def arrivals(src_rank, calls):
        return calls * bits(topo.mask(T.cores[src_rank], core))

    def quantise(q, s, tile, waits, done):
        for w, n in waits:
            g.vector.wait_ge(w, n)
        g.vector.quantize_mx(q, s, tile).then_inc(done, 1)

    def layer(k, wq, ws, waits, mq, ms, n, banks, tile, q, s):
        m0, m1, sc, ve, done = (T.sem[p + k] for p in ("m0", "m1", "sc", "ve", "k"))
        z0, z1 = banks
        for w, c in waits:
            g.tensor.wait_ge(w, c)
        g.tensor.matmul_mx(z0[:, 0:n], wq[:, 0:128], ws[:, 0:128], mq, ms, True, True).then_inc(m0, 1)
        g.tensor.matmul_mx(z1[:, 0:n], wq[:, 128:256], ws[:, 128:256], mq, ms, True, True).then_inc(m1, 1)
        relu = ActivationFunctionType.Relu
        g.scalar.wait_ge(m0, 1)
        g.scalar.activation(tile[:, 0:4 * n:4], z0[:, 0:n], relu, scale=C).then_inc(sc, 1)
        g.scalar.activation(tile[:, 1:4 * n:4], z0[:, 0:n], relu, scale=-C).then_inc(sc, 1)
        g.vector.wait_ge(m1, 1)
        g.vector.tensor_scalar(tile[:, 2:4 * n:4], z1[:, 0:n], C, 0.0, AluOpType.mult, AluOpType.max).then_inc(ve, 1)
        g.vector.tensor_scalar(tile[:, 3:4 * n:4], z1[:, 0:n], -C, 0.0, AluOpType.mult, AluOpType.max).then_inc(ve, 1)
        quantise(q, s, tile[:, 0:4 * n], [(sc, 2), (ve, 2)], done)

    def make_h():
        quantise(T.qx[:], T.sx[:], T.bx[:], [(sem.lx, 16)], sem.kx)
        quantise(T.qw1[:], T.sw1[:], T.bw1[:], [(sem.lw1, 16)], sem.kw1)
        a, b = 128 * rank, 128 * rank + 128
        layer("h", T.qw1, T.sw1, [(sem.kx, 1), (sem.kw1, 1)], T.qx[:], T.sx[:], 128, (T.ph0, T.ph1), T.th,
              T.hq[:, a:b], T.hs[:, a:b])

    def q_pw():
        quantise(T.qpw[:], T.spw[:], T.bpw[:], [(sem.lpw, 16)], sem.kpw)

    def q_w2():
        quantise(T.qw2[:], T.sw2[:], T.bw2[:], [(sem.lw2, 16)], sem.kw2)

    def send_h(ranks):
        a, b = 128 * rank, 128 * rank + 128
        hsem = T.sem["h%d" % rank]
        send(u8(T.hq[:, a:b]), u8(T.hq[:, a:b]), ranks, hsem)
        send(T.hs[:, a:b], T.hs[:, a:b], ranks, hsem)

    def make_y():
        copy = ActivationFunctionType.Copy
        g.tensor.wait_ge(sem.kw2, 1)
        g.tensor.wait_ge(sem.kh, 1)
        for j in range(4):
            if j != rank:
                g.tensor.wait_ge(T.sem["h%d" % j], arrivals(j, 2))
        g.tensor.matmul_mx(T.py0[:, 0:256], T.qw2[:], T.sw2[:], T.hq[:, 0:256], T.hs[:, 0:256], True, True).then_inc(sem.my0, 1)
        g.tensor.matmul_mx(T.py1[:, 0:256], T.qw2[:], T.sw2[:], T.hq[:, 256:512], T.hs[:, 256:512], True, True).then_inc(sem.my1, 1)
        g.scalar.wait_ge(sem.my0, 1)
        g.scalar.activation(T.ysb[:, 0:256], T.py0[:, 0:256], copy).then_inc(sem.cy, 1)
        g.vector.wait_ge(sem.my1, 1)
        g.vector.tensor_copy(T.ysb[:, 256:512], T.py1[:, 0:256]).then_inc(sem.cy, 1)
        g.sync.wait_ge(sem.cy, 2)
        g.sync.dma_start(T.y[:], T.ysb[:]).then_inc(sem.sty, 16)

    def load(queue, dst, src, s):
        queue.dma_start(dst, src).then_inc(s, 16)

    if rank == LAST:
        load(g.sync, T.bpx[:, 0:4 * H], T.px[:, 0:4 * H], sem.lpxa)
        load(g.scalar, T.bpx[:, 4 * H:8 * H], T.px[:, 4 * H:8 * H], sem.lpxb)
        load(g.sync, T.bx[:], T.x[:], sem.lx)
        load(g.scalar, T.bw1[:], T.w1[:], sem.lw1)
        quantise(T.qpx[:, 0:H], T.spx[:, 0:H], T.bpx[:, 0:4 * H], [(sem.lpxa, 16)], sem.kpxa)
        quantise(T.qpx[:, H:2 * H], T.spx[:, H:2 * H], T.bpx[:, 4 * H:8 * H], [(sem.lpxb, 16)], sem.kpxb)
        g.wait_ge(sem.kpxa, 1)
        left = send(u8(T.qpx[:, 0:H]), u8(T.rq[:, 0:H]), [0], sem.ina, sem.senta)
        g.wait_ge(sem.kpxb, 1)
        left += send(T.spx[:], T.rs[:], [0], sem.ins, sem.senta)
        left += send(u8(T.qpx[:, H:2 * H]), u8(T.rq[:, H:2 * H]), [0], sem.inb, sem.senta)
        g.sync.wait_ge(sem.senta, left)
        load(g.sync, T.bw2[:], T.w2[:], sem.lw2)
        load(g.sync, T.bpw[:], T.pw[:], sem.lpw)
        make_h()
        g.wait_ge(sem.kh, 1)
        send_h([1, 2, 0])
        q_w2()
        q_pw()
        make_y()
        copy = ActivationFunctionType.Copy
        g.tensor.wait_ge(sem.kpw, 1)
        for half, (src, arr, banks, mz) in enumerate(((1, sem.ina, (T.pa0, T.pa1), (sem.mz0, sem.mz1)),
                                                      (2, sem.inb, (T.pb0, T.pb1), (sem.mz2, sem.mz3)))):
            c0, c1 = H * half, H * half + H
            g.tensor.wait_ge(arr, arrivals(src, 2))
            for i in range(2):
                g.tensor.matmul_mx(banks[i][:, 0:H], T.qpw[:, 128 * i:128 * i + 128], T.spw[:, 128 * i:128 * i + 128],
                                   T.rq[:, c0:c1], T.rs[:, c0:c1], True, True).then_inc(mz[i], 1)
            g.scalar.wait_ge(mz[0], 1)
            g.vector.wait_ge(mz[1], 1)
            for m in range(3):
                a, b = max(c0, 128 * m), min(c1, 128 * m + 128)
                if a >= b:
                    continue
                done = sem.cza if m == 0 else sem.czb
                for i in range(2):
                    o = 128 * (2 * m + i) - 128 * m
                    out, z = T.zsb[:, o + a:o + b], banks[i][:, a - c0:b - c0]
                    if i == 0:
                        g.scalar.activation(out, z, copy).then_inc(done, 1)
                    else:
                        g.vector.tensor_copy(out, z).then_inc(done, 1)
        g.sync.wait_ge(sem.cza, 2)
        g.sync.dma_start(T.z[:, 0:256], T.zsb[:, 0:256]).then_inc(sem.stz, 16)
        g.sync.wait_ge(sem.czb, 6)
        g.sync.dma_start(T.z[:, 256:768], T.zsb[:, 256:768]).then_inc(sem.stz, 16)
        g.sync.wait_ge(sem.stz, 32)
    elif rank == 0:
        load(g.sync, T.bx[:], T.x[:], sem.lx)
        load(g.scalar, T.bw1[:], T.w1[:], sem.lw1)
        load(g.sync, T.bpw[:], T.pw[:], sem.lpw)
        load(g.sync, T.bw2[:], T.w2[:], sem.lw2)
        make_h()
        q_pw()
        g.wait_ge(sem.kh, 1)
        send_h([LAST])
        halves = (("a", [(sem.kpw, 1), (sem.ina, arrivals(LAST, 1)), (sem.ins, arrivals(LAST, 1))],
                   (T.pa0, T.pa1), T.t0, T.q0, T.s0, 1, sem.ina),
                  ("b", [(sem.inb, arrivals(LAST, 1))],
                   (T.pb0, T.pb1), T.t1, T.q1, T.s1, 2, sem.inb))
        for half, (k, waits, banks, t, q, s, to, rsem) in enumerate(halves):
            c0, c1 = H * half, H * half + H
            layer(k, T.qpw, T.spw, waits, T.rq[:, c0:c1], T.rs[:, c0:c1], H, banks, t, q[:], s[:])
            g.wait_ge(T.sem["k" + k], 1)
            send(u8(q[:]), u8(T.rq[:, c0:c1]), [to], rsem)
            send(s[:], T.rs[:, c0:c1], [to], rsem)
        send_h([1, 2])
        q_w2()
        make_y()
    else:
        other = 3 - rank
        c0, c1 = H * (rank - 1), H * rank
        arr = sem.ina if rank == 1 else sem.inb
        load(g.sync, T.bpw[:], T.pw[:], sem.lpw)
        load(g.scalar, T.bx[:], T.x[:], sem.lx)
        load(g.scalar, T.bw1[:], T.w1[:], sem.lw1)
        load(g.sync, T.bw2[:], T.w2[:], sem.lw2)
        q_pw()
        g.wait_ge(sem.kpw, 1)
        send(u8(T.qpw[:]), u8(T.rpw[:]), [other], sem.inw)
        send(T.spw[:], T.rspw[:], [other], sem.inw)
        make_h()
        g.wait_ge(sem.kh, 1)
        send_h([LAST, other])
        send_h([0])
        q_w2()
        own, foreign = (T.qpw, T.spw, (sem.kpw, 1)), (T.rpw, T.rspw, (sem.inw, arrivals(other, 2)))
        first, second = (own, foreign) if rank == 1 else (foreign, own)
        layer("a", first[0], first[1], [first[2], (arr, arrivals(0, 2))], T.rq[:, c0:c1], T.rs[:, c0:c1], H,
              (T.pa0, T.pa1), T.t0, T.q0[:], T.s0[:])
        layer("b", second[0], second[1], [second[2], (sem.ka, 1)], T.q0[:], T.s0[:], H,
              (T.pb0, T.pb1), T.t1, T.q1[:], T.s1[:])
        g.wait_ge(sem.kb, 1)
        send(u8(T.q1[:]), u8(T.rq[:, c0:c1]), [LAST], arr)
        send(T.s1[:], T.rs[:, c0:c1], [LAST], arr)
        make_y()
    g.sync.wait_ge(sem.sty, 16)
    g.wait_ge(sem.sent, nsent[0])
